import numpy as np
import ml_dtypes


def mxq(x, axis, fmt="e4m3"):
    dtype, down = {"e4m3": (ml_dtypes.float8_e4m3fn, 7), "e5m2": (ml_dtypes.float8_e5m2, 14)}[fmt]
    v = np.moveaxis(np.asarray(x, np.float32).astype(ml_dtypes.bfloat16).astype(np.float64), axis, -1)
    blocks = v.reshape(v.shape[:-1] + (-1, 32))
    amax = np.abs(blocks).max(-1, keepdims=True)
    byte = np.maximum(np.where(amax > 0, np.frexp(amax)[1] - 1 + 127, 0) - down, 1)
    scale = np.exp2(byte - 127.0)
    codes = (blocks / scale).astype(np.float32).astype(dtype).astype(np.float64)
    return np.moveaxis((codes * scale).reshape(v.shape), -1, axis)


WIDE = False


def mx_kscale(k):
    if not WIDE:
        return np.ones(k)
    levels = np.array([30, -30])
    if k % 512:
        return np.exp2(np.random.permutation(np.resize(levels, k // 32))).repeat(32)
    a = np.empty((k // 512, 16))
    for p in range(k // 512):
        a[p, :8] = np.random.permutation(np.resize(levels, 8))
        for g in range(8):
            far = levels[np.abs(levels - a[p, g]) >= 10]
            a[p, g + 8] = far[np.random.randint(len(far))]
    return np.exp2(a.ravel()).repeat(32)


def f64(x):
    return np.asarray(x).astype(np.float64)


def striped(idx):
    return np.tile(np.asarray(idx).reshape(-1, 16).T, (8, 1)).astype(np.uint16)


def unstriped(offs):
    return offs[:16].T.reshape(-1).astype(np.int64)


E2M1 = np.array([0.0, 0.5, 1.0, 1.5, 2.0, 3.0, 4.0, 6.0, -0.0, -0.5, -1.0, -1.5, -2.0, -3.0, -4.0, -6.0])


def pack_weight(w, fmt):
    k, n = w.shape
    w = f64(np.asarray(w, np.float32).astype(ml_dtypes.bfloat16)).reshape(k // 32, 32, n)
    amax = np.abs(w).max(1)
    if fmt in ("e4m3", "e5m2"):
        byte = np.frexp(amax)[1] - 1 + 127 - (7 if fmt == "e4m3" else 14)
    else:
        mant, ex = np.frexp(amax / 6.0)
        byte = np.where(mant > 0.5, ex, ex - 1) + 127
    byte = np.clip(np.where(amax > 0, byte, 1), 1, 254)
    scaled = (w * np.exp2(127.0 - byte)[:, None, :]).reshape(k, n).astype(np.float32)
    by_word = np.ascontiguousarray(scaled.reshape(k // 512, 128, 4, n).transpose(0, 1, 3, 2))
    if fmt in ("e4m3", "e5m2"):
        words = by_word.astype(ml_dtypes.float8_e4m3fn if fmt == "e4m3" else ml_dtypes.float8_e5m2).view(np.uint8)
    else:
        c = by_word.astype(ml_dtypes.float4_e2m1fn).view(np.uint8) & 0xF
        words = (c[..., 0::2] | (c[..., 1::2] << 4)).reshape(k // 512, 128, 2 * n)
    return np.ascontiguousarray(words), np.ascontiguousarray(byte.astype(np.uint8).reshape(k // 512, 16, n))


def unpack_weight(words, scales, fmt):
    g, _, n = scales.shape
    words = np.ascontiguousarray(words).reshape(g, 128, n, -1)
    if fmt in ("e4m3", "e5m2"):
        vals = words.view(ml_dtypes.float8_e4m3fn if fmt == "e4m3" else ml_dtypes.float8_e5m2).astype(np.float64)
    else:
        nib = np.empty((g, 128, n, 4), np.uint8)
        nib[..., 0::2] = words & 0xF
        nib[..., 1::2] = words >> 4
        vals = E2M1[nib]
    vals = vals * np.repeat(np.exp2(scales.astype(np.float64) - 127.0), 8, axis=1)[..., None]
    return vals.transpose(0, 1, 3, 2).reshape(g * 512, n)


K, T, J, R, L, N = 1024, 1024, 256, 512, 512, 256


def setup_inputs():
    n = np.random.standard_normal
    idx = np.random.permutation(T)[:J]
    idx2 = np.random.permutation(T)[:J]
    fk = mx_kscale(K)
    fr = mx_kscale(R)
    fl = mx_kscale(L)
    wp = pack_weight(n((K, R)) * 1 / np.sqrt(K) * fk[:, None] * fr, "e5m2")
    sxp = pack_weight(n((L, J)) / fl[:, None], "e4m3")
    wsp = pack_weight(n((L, R)) * 1 / np.sqrt(L) * fl[:, None] * fr, "e4m3")
    return {
        "xf": (n((K, T))).astype(np.float32),
        "fk": (np.random.uniform(0.5, 2.0, (K, 1)) / fk[:, None]).astype(np.float32),
        "w_words": wp[0],
        "w_scales": wp[1],
        "sx_words": sxp[0],
        "sx_scales": sxp[1],
        "ws_words": wsp[0],
        "ws_scales": wsp[1],
        "wb": (n((R, N)) * 1 / np.sqrt(R) / fr[:, None]).astype(np.float32),
        "bi": (np.random.uniform(-0.5, 0.5, (1, N))).astype(np.float32),
        "offs": striped(idx),
        "offs2": striped(idx2),
    }


def reference(xf, fk, w_words, w_scales, sx_words, sx_scales, ws_words, ws_scales, wb, bi, offs, offs2):
    idx = unstriped(offs)
    idx2 = unstriped(offs2)
    wu = unpack_weight(w_words, w_scales, "e5m2")
    sxu = unpack_weight(sx_words, sx_scales, "e4m3")
    wsu = unpack_weight(ws_words, ws_scales, "e4m3")
    u = np.maximum(f64(xf)[:, idx], f64(xf)[:, idx2]) * f64(fk)
    uq = mxq(u, 0, "e4m3")
    a = wu.T @ uq
    b2 = wsu.T @ sxu
    hid = np.maximum(a, b2)
    hidq = mxq(hid, 0, "e5m2")
    wbq = mxq(f64(wb), 0, "e4m3")
    p = hidq.T @ wbq
    ea = np.exp(0.7 * p + f64(bi))
    y = 256.0 * ea / np.sum(ea, axis=1, keepdims=True)
    return y

@@ -1,0 +1,220 @@
+from contextlib import ExitStack
+
+import concourse.mybir as mybir
+from concourse.masks import make_identity
+
+K, T, J, R, L, N = 1024, 1024, 256, 512, 512, 256
+FLOPS = 2 * (K * R * J + L * R * J + R * J * N)
+
+F32 = mybir.dt.float32
+BF16 = mybir.dt.bfloat16
+I32 = mybir.dt.int32
+U16 = mybir.dt.uint16
+U8 = mybir.dt.uint8
+E4M3 = mybir.dt.float8_e4m3fn_x4
+E5M2 = mybir.dt.float8_e5m2_x4
+ALU = mybir.AluOpType
+ACT = mybir.ActivationFunctionType
+
+P = 128
+PACK = 4
+PASS = P * PACK
+PASSES = K // PASS
+PLANES = PASSES * PACK
+HALVES = J // P
+RUN = 4
+VECTOR_GATHERS = (0, 2, 4, 6, 7)
+
+
+def weave(copy, dst, src):
+    copy(
+        out=dst.rearrange("p (c i) t -> p c t i", i=RUN),
+        in_=src.rearrange("p t (c i) -> p c t i", i=RUN),
+    )
+
+
+def tile_list_largerpicks_rival_rowshares_kernel(
+    tc, xf, fk, w_words, w_scales, sx_words, sx_scales, ws_words, ws_scales, wb, bi, offs, offs2, out
+):
+    nc = tc.nc
+    with ExitStack() as ctx:
+        keep = ctx.enter_context(tc.tile_pool(name="keep", bufs=1))
+        psum = ctx.enter_context(tc.psum_pool(name="psum", bufs=1))
+
+        list_a = keep.tile([P, J // 16], U16, name="list_a")
+        list_b = keep.tile([P, J // 16], U16, name="list_b")
+        planes = [keep.tile([P, T], F32, name=f"plane{i}") for i in range(PLANES)]
+        factor = keep.tile([P, PASSES, PACK], F32, name="factor")
+        bias_col = keep.tile([P, 2], F32, name="bias_col")
+        given_scales = keep.tile([P, PASSES * R + R + J], U8, name="given_scales", align_bytes=64)
+        w_codes = [keep.tile([P, R], I32, name=f"w_codes{a}", align_bytes=64) for a in range(PASSES)]
+        ws_codes = keep.tile([P, R], I32, name="ws_codes", align_bytes=64)
+        sx_codes = keep.tile([P, J], I32, name="sx_codes", align_bytes=64)
+        wb_raw = keep.tile([P, PACK, N], F32, name="wb_raw")
+        ident = keep.tile([P, P], F32, name="ident")
+
+        nc.vector.memset(given_scales[:].bitcast(I32), 0)
+        make_identity(nc, ident[:])
+
+        ws_at = PASSES * R
+        sx_at = ws_at + R
+
+        def scale_loads():
+            loads = []
+            for src, at, width in ((ws_scales, ws_at, R), (sx_scales, sx_at, J), (w_scales, 0, R)):
+                passes = src.shape[0]
+                for q in range(4):
+                    dst = given_scales[32 * q : 32 * q + 4, at : at + passes * width].bitcast(I32)
+                    loads.append(
+                        (
+                            dst.rearrange("r (z c) -> r z c", z=passes),
+                            src[:, 4 * q : 4 * q + 4, :].bitcast(I32).rearrange("z r c -> r z c"),
+                        )
+                    )
+            return loads
+
+        def words(src):
+            return src.rearrange("p c t -> p (c t)").bitcast(I32)
+
+        xf_planes = xf.rearrange("(a p t) n -> a t p n", p=P, t=PACK)
+        small = scale_loads()
+        for i in range(PLANES):
+            nc.sync.dma_start(out=planes[i][:], in_=xf_planes[i // PACK, i % PACK])
+            if i == 0:
+                nc.sync.dma_start(list_a[:], offs)
+                nc.sync.dma_start(list_b[:], offs2)
+                nc.sync.dma_start(out=factor[:], in_=fk.rearrange("(a p t) o -> p a (t o)", p=P, t=PACK))
+                nc.sync.dma_start(out=bias_col[:], in_=bi.rearrange("o (p e) -> p (o e)", e=2))
+            elif i >= 2:
+                for dst, src in small[2 * (i - 2) : 2 * (i - 1)]:
+                    nc.sync.dma_start(out=dst, in_=src)
+        nc.sync.dma_start(out=ws_codes[:], in_=words(ws_words[0]))
+        nc.sync.dma_start(out=sx_codes[:], in_=words(sx_words[0]))
+        for a in range(PASSES):
+            nc.sync.dma_start(out=w_codes[a][:], in_=words(w_words[a]))
+        nc.sync.dma_start(out=wb_raw[:], in_=wb.rearrange("(p t) n -> p t n", t=PACK))
+
+        bias_ps = psum.tile([P, 2, P], F32, name="bias_ps", tag="turn0")
+        for e in range(2):
+            nc.tensor.transpose(bias_ps[:, e, :], bias_col[:, e : e + 1].to_broadcast([P, P]), ident[:])
+        bias_row = keep.tile([P, P, 2], F32, name="bias_row")
+        nc.vector.tensor_copy(out=bias_row[:], in_=bias_ps[:].rearrange("p e n -> p n e"))
+
+        a_ps = [psum.tile([P, R], F32, name=f"a_ps{h}") for h in range(HALVES)]
+        for a in range(PASSES):
+            woven = keep.tile([P, J, PACK], BF16, name=f"u_woven{a}", align_bytes=64)
+            for t in range(PACK):
+                i = a * PACK + t
+                cuts = HALVES if i == PLANES - 1 else 1
+                width = J // cuts
+                picks = []
+                for c in range(cuts):
+                    cols = slice(c * width // 16, (c + 1) * width // 16)
+                    pick_a = keep.tile([P, width], F32, name=f"pick_a{i}{c}", tag=f"pick_a{i}{c}", align_bytes=64)
+                    pick_b = keep.tile([P, width], F32, name=f"pick_b{i}{c}", tag=f"pick_b{i}{c}", align_bytes=64)
+                    nc.scalar.activation(pick_a[:], planes[i][:].indirect(list_a[:, cols]), ACT.Copy)
+                    if i in VECTOR_GATHERS:
+                        nc.vector.tensor_copy(pick_b[:], planes[i][:].indirect(list_b[:, cols]))
+                    else:
+                        nc.scalar.activation(pick_b[:], planes[i][:].indirect(list_b[:, cols]), ACT.Copy)
+                    picks.append((pick_a, pick_b))
+                larger = keep.tile([P, J], F32, name=f"larger{i}")
+                for c in range(cuts):
+                    nc.vector.tensor_tensor(
+                        larger[:, c * width : (c + 1) * width], picks[c][0][:], picks[c][1][:], ALU.max
+                    )
+                for c in range(cuts):
+                    cols = slice(c * width, (c + 1) * width)
+                    nc.vector.tensor_scalar(
+                        woven[:, cols, t], larger[:, cols], factor[:, a, t : t + 1], None, ALU.mult
+                    )
+            for h in range(HALVES):
+                u_codes = keep.tile([P, P], I32, name=f"u_codes{a}{h}", align_bytes=64)
+                u_scales = keep.tile([P, P], U8, name=f"u_scales{a}{h}", align_bytes=64)
+                nc.vector.quantize_mx(
+                    out=u_codes[:].bitcast(E4M3), scales=u_scales[:], in_=woven[:, h * P : (h + 1) * P, :].rearrange("p c t -> p (c t)")
+                )
+                nc.tensor.matmul_mx(
+                    out=a_ps[h][:],
+                    lhsT=u_codes[:].bitcast(E4M3),
+                    lhsT_scale=u_scales[:],
+                    rhs=w_codes[a][:].bitcast(E5M2),
+                    rhs_scale=given_scales[:, a * R : (a + 1) * R],
+                    start=(a == 0),
+                    stop=(a == PASSES - 1),
+                )
+
+        rival = []
+        for h in range(HALVES):
+            b_ps = psum.tile([P, R], F32, name=f"b_ps{h}")
+            nc.tensor.matmul_mx(
+                out=b_ps[:],
+                lhsT=sx_codes[:, h * P : (h + 1) * P].bitcast(E4M3),
+                lhsT_scale=given_scales[:, sx_at + h * P : sx_at + (h + 1) * P],
+                rhs=ws_codes[:].bitcast(E4M3),
+                rhs_scale=given_scales[:, ws_at : ws_at + R],
+                start=True,
+                stop=True,
+            )
+            b_sb = keep.tile([P, 2, P, 2], F32, name=f"b_sb{h}", tag=f"pick_a{PLANES - 1}{h}", align_bytes=64)
+            nc.scalar.copy(out=b_sb[:], in_=b_ps[:].rearrange("j (p u e) -> j u p e", u=2, e=2))
+            rival.append(b_sb)
+
+        wb_woven = keep.tile([P, N, PACK], BF16, name="wb_woven", tag=f"pick_b{PLANES - 1}1", align_bytes=64)
+        weave(nc.scalar.copy, wb_woven[:], wb_raw[:])
+        wb_codes = keep.tile([P, N], I32, name="wb_codes", align_bytes=64)
+        wb_scales = keep.tile([P, N], U8, name="wb_scales", align_bytes=64)
+
+        hid_woven = []
+        for h in range(HALVES):
+            hid = keep.tile([P, 2, P, 2], BF16, name=f"hid{h}")
+            turned = psum.tile([P, 2, P], F32, name=f"turned{h}", tag=f"turn{h}")
+            a_view = a_ps[h][:].rearrange("j (p u e) -> j u p e", u=2, e=2)
+            for u in range(2):
+                nc.vector.tensor_tensor(hid[:, u], a_view[:, u], rival[h][:, u], ALU.max)
+                nc.tensor.transpose(
+                    turned[:, u, :], hid[:, u].rearrange("j p e -> j (p e)").bitcast(F32), ident[:]
+                )
+            hw = keep.tile([P, P * PACK], BF16, name=f"hid_woven{h}", align_bytes=64)
+            nc.scalar.copy(
+                out=hw[:].bitcast(F32).rearrange("p (j u) -> p j u", u=2),
+                in_=turned[:].rearrange("p u j -> p j u"),
+            )
+            hid_woven.append(hw)
+
+        nc.vector.quantize_mx(
+            out=wb_codes[:].bitcast(E4M3), scales=wb_scales[:], in_=wb_woven[:].rearrange("p c t -> p (c t)")
+        )
+
+        p_ps = []
+        for h in range(HALVES):
+            hid_codes = keep.tile([P, P], I32, name=f"hid_codes{h}", align_bytes=64)
+            hid_scales = keep.tile([P, P], U8, name=f"hid_scales{h}", align_bytes=64)
+            nc.vector.quantize_mx(out=hid_codes[:].bitcast(E5M2), scales=hid_scales[:], in_=hid_woven[h][:])
+            pp = psum.tile([P, N], F32, name=f"p_ps{h}")
+            nc.tensor.matmul_mx(
+                out=pp[:],
+                lhsT=hid_codes[:].bitcast(E5M2),
+                lhsT_scale=hid_scales[:],
+                rhs=wb_codes[:].bitcast(E4M3),
+                rhs_scale=wb_scales[:],
+                start=True,
+                stop=True,
+            )
+            p_ps.append(pp)
+
+        for h in range(HALVES):
+            neg = keep.tile([P, N], F32, name=f"neg{h}")
+            least = keep.tile([P, 1], F32, name=f"least{h}")
+            ea = keep.tile([P, N], F32, name=f"ea{h}")
+            total = keep.tile([P, 1], F32, name=f"total{h}")
+            inv = keep.tile([P, 1], F32, name=f"inv{h}")
+            shares = keep.tile([P, N], F32, name=f"shares{h}")
+            nc.vector.scalar_tensor_tensor(
+                neg[:], p_ps[h][:], -0.7, bias_row[:].rearrange("p n e -> p (n e)"), ALU.mult, ALU.subtract
+            )
+            nc.vector.tensor_reduce(least[:], neg[:], mybir.AxisListType.X, ALU.min)
+            nc.scalar.activation(ea[:], neg[:], ACT.Exp, bias=least[:], scale=-1.0, accum_out=total[:])
+            nc.vector.reciprocal(inv[:], total[:])
+            nc.vector.tensor_scalar(shares[:], ea[:], inv[:], 256.0, ALU.mult, ALU.mult)
+            nc.sync.dma_start(out=out[h * P : (h + 1) * P, :], in_=shares[:])

@@ -23,7 +23,7 @@ PASSES = K // PASS
 PLANES = PASSES * PACK
 HALVES = J // P
 RUN = 4
-VECTOR_GATHERS = (0, 2, 4, 6, 7)
+VECTOR_GATHERS = (0, 1, 2, 3, 6, 7)
 
 
 def weave(copy, dst, src):
@@ -55,6 +55,10 @@ def tile_list_largerpicks_rival_rowshares_kernel(
 
         nc.vector.memset(given_scales[:].bitcast(I32), 0)
         make_identity(nc, ident[:])
+        warm_in = keep.tile([P, 1], F32, name="warm_in")
+        warm_out = keep.tile([P, 1], F32, name="warm_out")
+        nc.vector.memset(warm_in[:], 0.0)
+        nc.scalar.activation(warm_out[:], warm_in[:], ACT.Copy)
 
         ws_at = PASSES * R
         sx_at = ws_at + R
@@ -77,16 +81,15 @@ def tile_list_largerpicks_rival_rowshares_kernel(
             return src.rearrange("p c t -> p (c t)").bitcast(I32)
 
         xf_planes = xf.rearrange("(a p t) n -> a t p n", p=P, t=PACK)
-        small = scale_loads()
+        small = [(bias_col[:], bi.rearrange("o (p e) -> p (o e)", e=2))] + scale_loads()
         for i in range(PLANES):
             nc.sync.dma_start(out=planes[i][:], in_=xf_planes[i // PACK, i % PACK])
             if i == 0:
                 nc.sync.dma_start(list_a[:], offs)
                 nc.sync.dma_start(list_b[:], offs2)
                 nc.sync.dma_start(out=factor[:], in_=fk.rearrange("(a p t) o -> p a (t o)", p=P, t=PACK))
-                nc.sync.dma_start(out=bias_col[:], in_=bi.rearrange("o (p e) -> p (o e)", e=2))
             elif i >= 2:
-                for dst, src in small[2 * (i - 2) : 2 * (i - 1)]:
+                for dst, src in small[2 * (i - 2) : 2 * (i - 1) if i < PLANES - 1 else None]:
                     nc.sync.dma_start(out=dst, in_=src)
         nc.sync.dma_start(out=ws_codes[:], in_=words(ws_words[0]))
         nc.sync.dma_start(out=sx_codes[:], in_=words(sx_words[0]))
@@ -98,50 +101,58 @@ def tile_list_largerpicks_rival_rowshares_kernel(
         for e in range(2):
             nc.tensor.transpose(bias_ps[:, e, :], bias_col[:, e : e + 1].to_broadcast([P, P]), ident[:])
         bias_row = keep.tile([P, P, 2], F32, name="bias_row")
-        nc.vector.tensor_copy(out=bias_row[:], in_=bias_ps[:].rearrange("p e n -> p n e"))
+        nc.scalar.copy(out=bias_row[:], in_=bias_ps[:].rearrange("p e n -> p n e"))
 
         a_ps = [psum.tile([P, R], F32, name=f"a_ps{h}") for h in range(HALVES)]
         for a in range(PASSES):
+            last_pass = a == PASSES - 1
+            col_cuts = [slice(h * P, (h + 1) * P) for h in range(HALVES)] if last_pass else [slice(0, J)]
+            pick_a = keep.tile([P, PACK, J], F32, name=f"pick_a{a}")
+            pick_b = keep.tile([P, PACK, J], F32, name=f"pick_b{a}")
+            larger = keep.tile([P, PACK, J], F32, name=f"larger{a}")
             woven = keep.tile([P, J, PACK], BF16, name=f"u_woven{a}", align_bytes=64)
+            u_codes = keep.tile([P, J], I32, name=f"u_codes{a}", align_bytes=64)
+            u_scales = keep.tile([P, J], U8, name=f"u_scales{a}", align_bytes=64)
             for t in range(PACK):
                 i = a * PACK + t
-                cuts = HALVES if i == PLANES - 1 else 1
-                width = J // cuts
-                picks = []
-                for c in range(cuts):
-                    cols = slice(c * width // 16, (c + 1) * width // 16)
-                    pick_a = keep.tile([P, width], F32, name=f"pick_a{i}{c}", tag=f"pick_a{i}{c}", align_bytes=64)
-                    pick_b = keep.tile([P, width], F32, name=f"pick_b{i}{c}", tag=f"pick_b{i}{c}", align_bytes=64)
-                    nc.scalar.activation(pick_a[:], planes[i][:].indirect(list_a[:, cols]), ACT.Copy)
+                cuts = col_cuts if t == PACK - 1 else [slice(0, J)]
+                for cols in cuts:
+                    entries = slice(cols.start // 16, cols.stop // 16)
+                    nc.scalar.activation(pick_a[:, t, cols], planes[i][:].indirect(list_a[:, entries]), ACT.Copy)
                     if i in VECTOR_GATHERS:
-                        nc.vector.tensor_copy(pick_b[:], planes[i][:].indirect(list_b[:, cols]))
+                        nc.vector.tensor_copy(pick_b[:, t, cols], planes[i][:].indirect(list_b[:, entries]))
                     else:
-                        nc.scalar.activation(pick_b[:], planes[i][:].indirect(list_b[:, cols]), ACT.Copy)
-                    picks.append((pick_a, pick_b))
-                larger = keep.tile([P, J], F32, name=f"larger{i}")
-                for c in range(cuts):
-                    nc.vector.tensor_tensor(
-                        larger[:, c * width : (c + 1) * width], picks[c][0][:], picks[c][1][:], ALU.max
-                    )
-                for c in range(cuts):
-                    cols = slice(c * width, (c + 1) * width)
-                    nc.vector.tensor_scalar(
-                        woven[:, cols, t], larger[:, cols], factor[:, a, t : t + 1], None, ALU.mult
-                    )
-            for h in range(HALVES):
-                u_codes = keep.tile([P, P], I32, name=f"u_codes{a}{h}", align_bytes=64)
-                u_scales = keep.tile([P, P], U8, name=f"u_scales{a}{h}", align_bytes=64)
-                nc.vector.quantize_mx(
-                    out=u_codes[:].bitcast(E4M3), scales=u_scales[:], in_=woven[:, h * P : (h + 1) * P, :].rearrange("p c t -> p (c t)")
+                        nc.scalar.activation(pick_b[:, t, cols], planes[i][:].indirect(list_b[:, entries]), ACT.Copy)
+                if t % 2 == 1:
+                    pair = slice(t - 1, t + 1)
+                    for cols in cuts:
+                        nc.vector.tensor_tensor(
+                            larger[:, pair, cols], pick_a[:, pair, cols], pick_b[:, pair, cols], ALU.max
+                        )
+            for cols in col_cuts:
+                width = cols.stop - cols.start
+                nc.vector.tensor_tensor(
+                    woven[:, cols, :].rearrange("p (c i) t -> p c t i", i=RUN),
+                    larger[:, :, cols].rearrange("p t (c i) -> p c t i", i=RUN),
+                    factor[:, a, :].unsqueeze(1).unsqueeze(3).to_broadcast([P, width // RUN, PACK, RUN]),
+                    ALU.mult,
                 )
+            for cols in col_cuts:
+                nc.vector.quantize_mx(
+                    out=u_codes[:, cols].bitcast(E4M3),
+                    scales=u_scales[:, cols],
+                    in_=woven[:, cols, :].rearrange("p c t -> p (c t)"),
+                )
+            for h in range(HALVES):
+                cols = slice(h * P, (h + 1) * P)
                 nc.tensor.matmul_mx(
                     out=a_ps[h][:],
-                    lhsT=u_codes[:].bitcast(E4M3),
-                    lhsT_scale=u_scales[:],
+                    lhsT=u_codes[:, cols].bitcast(E4M3),
+                    lhsT_scale=u_scales[:, cols],
                     rhs=w_codes[a][:].bitcast(E5M2),
                     rhs_scale=given_scales[:, a * R : (a + 1) * R],
                     start=(a == 0),
-                    stop=(a == PASSES - 1),
+                    stop=last_pass,
                 )
 
         rival = []
@@ -156,11 +167,11 @@ def tile_list_largerpicks_rival_rowshares_kernel(
                 start=True,
                 stop=True,
             )
-            b_sb = keep.tile([P, 2, P, 2], F32, name=f"b_sb{h}", tag=f"pick_a{PLANES - 1}{h}", align_bytes=64)
+            b_sb = keep.tile([P, 2, P, 2], F32, name=f"b_sb{h}")
             nc.scalar.copy(out=b_sb[:], in_=b_ps[:].rearrange("j (p u e) -> j u p e", u=2, e=2))
             rival.append(b_sb)
 
-        wb_woven = keep.tile([P, N, PACK], BF16, name="wb_woven", tag=f"pick_b{PLANES - 1}1", align_bytes=64)
+        wb_woven = keep.tile([P, N, PACK], BF16, name="wb_woven", align_bytes=64)
         weave(nc.scalar.copy, wb_woven[:], wb_raw[:])
         wb_codes = keep.tile([P, N], I32, name="wb_codes", align_bytes=64)
         wb_scales = keep.tile([P, N], U8, name="wb_scales", align_bytes=64)

@@ -46,55 +46,59 @@ def tile_list_largerpicks_rival_rowshares_kernel(
         planes = [keep.tile([P, T], F32, name=f"plane{i}") for i in range(PLANES)]
         factor = keep.tile([P, PASSES, PACK], F32, name="factor")
         bias_col = keep.tile([P, 2], F32, name="bias_col")
-        given_scales = keep.tile([P, PASSES * R + R + J], U8, name="given_scales", align_bytes=64)
+        rival_scales = keep.tile([P, R + J], U8, name="rival_scales", align_bytes=64)
+        w_plane = keep.tile([P, PASSES * R], U8, name="w_plane", align_bytes=64)
         w_codes = [keep.tile([P, R], I32, name=f"w_codes{a}", align_bytes=64) for a in range(PASSES)]
         ws_codes = keep.tile([P, R], I32, name="ws_codes", align_bytes=64)
         sx_codes = keep.tile([P, J], I32, name="sx_codes", align_bytes=64)
         wb_raw = keep.tile([P, PACK, N], F32, name="wb_raw")
         ident = keep.tile([P, P], F32, name="ident")
 
-        nc.vector.memset(given_scales[:].bitcast(I32), 0)
+        nc.vector.memset(rival_scales[:].bitcast(I32), 0)
+        nc.vector.memset(w_plane[:].bitcast(I32), 0)
         make_identity(nc, ident[:])
         warm_in = keep.tile([P, 1], F32, name="warm_in")
         warm_out = keep.tile([P, 1], F32, name="warm_out")
         nc.vector.memset(warm_in[:], 0.0)
         nc.scalar.activation(warm_out[:], warm_in[:], ACT.Copy)
+        ws_row, sx_row = 4, 8
 
-        ws_at = PASSES * R
-        sx_at = ws_at + R
-
-        def scale_loads():
-            loads = []
-            for src, at, width in ((ws_scales, ws_at, R), (sx_scales, sx_at, J), (w_scales, 0, R)):
-                passes = src.shape[0]
-                for q in range(4):
-                    dst = given_scales[32 * q : 32 * q + 4, at : at + passes * width].bitcast(I32)
-                    loads.append(
-                        (
-                            dst.rearrange("r (z c) -> r z c", z=passes),
-                            src[:, 4 * q : 4 * q + 4, :].bitcast(I32).rearrange("z r c -> r z c"),
-                        )
-                    )
-            return loads
+        def scale_loads(src, plane, row):
+            passes = src.shape[0]
+            return [
+                (
+                    plane[32 * q + row : 32 * q + row + 4, :].bitcast(I32).rearrange("r (z c) -> r z c", z=passes),
+                    src[:, 4 * q : 4 * q + 4, :].bitcast(I32).rearrange("z r c -> r z c"),
+                )
+                for q in range(4)
+            ]
 
         def words(src):
             return src.rearrange("p c t -> p (c t)").bitcast(I32)
 
         xf_planes = xf.rearrange("(a p t) n -> a t p n", p=P, t=PACK)
-        small = [(bias_col[:], bi.rearrange("o (p e) -> p (o e)", e=2))] + scale_loads()
+        small = (
+            [(factor[:], fk.rearrange("(a p t) o -> p a (t o)", p=P, t=PACK))]
+            + scale_loads(ws_scales, rival_scales[:, :R], ws_row)
+            + scale_loads(sx_scales, rival_scales[:, R:], sx_row)
+            + [(bias_col[:], bi.rearrange("o (p e) -> p (o e)", e=2))]
+        )
+        behind = (1, 1, 1, 1, 2, 1, 1, 2)
+        at = 0
         for i in range(PLANES):
             nc.sync.dma_start(out=planes[i][:], in_=xf_planes[i // PACK, i % PACK])
             if i == 0:
                 nc.sync.dma_start(list_a[:], offs)
                 nc.sync.dma_start(list_b[:], offs2)
-                nc.sync.dma_start(out=factor[:], in_=fk.rearrange("(a p t) o -> p a (t o)", p=P, t=PACK))
-            elif i >= 2:
-                for dst, src in small[2 * (i - 2) : 2 * (i - 1) if i < PLANES - 1 else None]:
-                    nc.sync.dma_start(out=dst, in_=src)
+            for dst, src in small[at : at + behind[i]]:
+                nc.sync.dma_start(out=dst, in_=src)
+            at = at + behind[i]
         nc.sync.dma_start(out=ws_codes[:], in_=words(ws_words[0]))
         nc.sync.dma_start(out=sx_codes[:], in_=words(sx_words[0]))
-        for a in range(PASSES):
-            nc.sync.dma_start(out=w_codes[a][:], in_=words(w_words[a]))
+        nc.sync.dma_start(out=w_codes[0][:], in_=words(w_words[0]))
+        for dst, src in scale_loads(w_scales, w_plane[:], 0):
+            nc.sync.dma_start(out=dst, in_=src)
+        nc.sync.dma_start(out=w_codes[1][:], in_=words(w_words[1]))
         nc.sync.dma_start(out=wb_raw[:], in_=wb.rearrange("(p t) n -> p t n", t=PACK))
 
         bias_ps = psum.tile([P, 2, P], F32, name="bias_ps", tag="turn0")
@@ -102,6 +106,18 @@ def tile_list_largerpicks_rival_rowshares_kernel(
             nc.tensor.transpose(bias_ps[:, e, :], bias_col[:, e : e + 1].to_broadcast([P, P]), ident[:])
         bias_row = keep.tile([P, P, 2], F32, name="bias_row")
         nc.scalar.copy(out=bias_row[:], in_=bias_ps[:].rearrange("p e n -> p n e"))
+
+        b_ps = [psum.tile([P, R], F32, name=f"b_ps{h}") for h in range(HALVES)]
+        for h in range(HALVES):
+            nc.tensor.matmul_mx(
+                out=b_ps[h][:],
+                lhsT=sx_codes[:, h * P : (h + 1) * P].bitcast(E4M3),
+                lhsT_scale=rival_scales[sx_row:, R + h * P : R + (h + 1) * P],
+                rhs=ws_codes[:].bitcast(E4M3),
+                rhs_scale=rival_scales[ws_row:, :R],
+                start=True,
+                stop=True,
+            )
 
         a_ps = [psum.tile([P, R], F32, name=f"a_ps{h}") for h in range(HALVES)]
         for a in range(PASSES):
@@ -119,7 +135,7 @@ def tile_list_largerpicks_rival_rowshares_kernel(
                 for cols in cuts:
                     entries = slice(cols.start // 16, cols.stop // 16)
                     nc.scalar.activation(pick_a[:, t, cols], planes[i][:].indirect(list_a[:, entries]), ACT.Copy)
-                    if i in VECTOR_GATHERS:
+                    if i in VECTOR_GATHERS and cols.start == 0:
                         nc.vector.tensor_copy(pick_b[:, t, cols], planes[i][:].indirect(list_b[:, entries]))
                     else:
                         nc.scalar.activation(pick_b[:, t, cols], planes[i][:].indirect(list_b[:, entries]), ACT.Copy)
@@ -150,29 +166,20 @@ def tile_list_largerpicks_rival_rowshares_kernel(
                     lhsT=u_codes[:, cols].bitcast(E4M3),
                     lhsT_scale=u_scales[:, cols],
                     rhs=w_codes[a][:].bitcast(E5M2),
-                    rhs_scale=given_scales[:, a * R : (a + 1) * R],
+                    rhs_scale=w_plane[:, a * R : (a + 1) * R],
                     start=(a == 0),
                     stop=last_pass,
                 )
 
         rival = []
         for h in range(HALVES):
-            b_ps = psum.tile([P, R], F32, name=f"b_ps{h}")
-            nc.tensor.matmul_mx(
-                out=b_ps[:],
-                lhsT=sx_codes[:, h * P : (h + 1) * P].bitcast(E4M3),
-                lhsT_scale=given_scales[:, sx_at + h * P : sx_at + (h + 1) * P],
-                rhs=ws_codes[:].bitcast(E4M3),
-                rhs_scale=given_scales[:, ws_at : ws_at + R],
-                start=True,
-                stop=True,
-            )
             b_sb = keep.tile([P, 2, P, 2], F32, name=f"b_sb{h}")
-            nc.scalar.copy(out=b_sb[:], in_=b_ps[:].rearrange("j (p u e) -> j u p e", u=2, e=2))
+            nc.scalar.copy(out=b_sb[:], in_=b_ps[h][:].rearrange("j (p u e) -> j u p e", u=2, e=2))
             rival.append(b_sb)
 
         wb_woven = keep.tile([P, N, PACK], BF16, name="wb_woven", align_bytes=64)
-        weave(nc.scalar.copy, wb_woven[:], wb_raw[:])
+        weave(nc.vector.tensor_copy, wb_woven[:, : N // 2, :], wb_raw[:, :, : N // 2])
+        weave(nc.scalar.copy, wb_woven[:, N // 2 :, :], wb_raw[:, :, N // 2 :])
         wb_codes = keep.tile([P, N], I32, name="wb_codes", align_bytes=64)
         wb_scales = keep.tile([P, N], U8, name="wb_scales", align_bytes=64)
 

@@ -5,6 +5,8 @@ from concourse.masks import make_identity
 
 K, T, J, R, L, N = 1024, 1024, 256, 512, 512, 256
 FLOPS = 2 * (K * R * J + L * R * J + R * J * N)
+LOGIT_SCALE = 0.7
+SHARE_SUM = 256.0
 
 F32 = mybir.dt.float32
 BF16 = mybir.dt.bfloat16
@@ -18,36 +20,59 @@ ACT = mybir.ActivationFunctionType
 
 P = 128
 PACK = 4
-PASS = P * PACK
-PASSES = K // PASS
+PASSES = K // (P * PACK)
 PLANES = PASSES * PACK
 HALVES = J // P
-RUN = 4
+LIST_ROWS = 16
+QUADRANTS = 4
+WS_ROW, SX_ROW = 4, 8
+RUN = 2
 VECTOR_GATHERS = (0, 1, 2, 3, 6, 7)
+SMALL_BEHIND_PLANE = (1, 1, 1, 1, 2, 1, 1, 2)
 
 
-def weave(copy, dst, src):
-    copy(
-        out=dst.rearrange("p (c i) t -> p c t i", i=RUN),
-        in_=src.rearrange("p t (c i) -> p c t i", i=RUN),
-    )
+def woven_order(ap):
+    return ap.rearrange("p (c i) t -> p c t i", i=RUN)
+
+
+def plane_order(ap):
+    return ap.rearrange("p t (c i) -> p c t i", i=RUN)
+
+
+def as_words(codes):
+    return codes.rearrange("p c t -> p (c t)").bitcast(I32)
+
+
+def scale_loads(src, scale_tile, first_row):
+    passes = src.shape[0]
+    return [
+        (
+            scale_tile[32 * q + first_row : 32 * q + first_row + 4, :]
+            .bitcast(I32)
+            .rearrange("r (z c) -> r z c", z=passes),
+            src[:, 4 * q : 4 * q + 4, :].bitcast(I32).rearrange("z r c -> r z c"),
+        )
+        for q in range(QUADRANTS)
+    ]
 
 
 def tile_list_largerpicks_rival_rowshares_kernel(
     tc, xf, fk, w_words, w_scales, sx_words, sx_scales, ws_words, ws_scales, wb, bi, offs, offs2, out
 ):
     nc = tc.nc
+    halves = [slice(h * P, (h + 1) * P) for h in range(HALVES)]
+    whole = [slice(0, J)]
     with ExitStack() as ctx:
         keep = ctx.enter_context(tc.tile_pool(name="keep", bufs=1))
         psum = ctx.enter_context(tc.psum_pool(name="psum", bufs=1))
 
-        list_a = keep.tile([P, J // 16], U16, name="list_a")
-        list_b = keep.tile([P, J // 16], U16, name="list_b")
+        list_a = keep.tile([P, J // LIST_ROWS], U16, name="list_a")
+        list_b = keep.tile([P, J // LIST_ROWS], U16, name="list_b")
         planes = [keep.tile([P, T], F32, name=f"plane{i}") for i in range(PLANES)]
         factor = keep.tile([P, PASSES, PACK], F32, name="factor")
         bias_col = keep.tile([P, 2], F32, name="bias_col")
         rival_scales = keep.tile([P, R + J], U8, name="rival_scales", align_bytes=64)
-        w_plane = keep.tile([P, PASSES * R], U8, name="w_plane", align_bytes=64)
+        w_scale_tile = keep.tile([P, PASSES * R], U8, name="w_scale_tile", align_bytes=64)
         w_codes = [keep.tile([P, R], I32, name=f"w_codes{a}", align_bytes=64) for a in range(PASSES)]
         ws_codes = keep.tile([P, R], I32, name="ws_codes", align_bytes=64)
         sx_codes = keep.tile([P, J], I32, name="sx_codes", align_bytes=64)
@@ -55,50 +80,36 @@ def tile_list_largerpicks_rival_rowshares_kernel(
         ident = keep.tile([P, P], F32, name="ident")
 
         nc.vector.memset(rival_scales[:].bitcast(I32), 0)
-        nc.vector.memset(w_plane[:].bitcast(I32), 0)
+        nc.vector.memset(w_scale_tile[:].bitcast(I32), 0)
         make_identity(nc, ident[:])
+
         warm_in = keep.tile([P, 1], F32, name="warm_in")
         warm_out = keep.tile([P, 1], F32, name="warm_out")
         nc.vector.memset(warm_in[:], 0.0)
         nc.scalar.activation(warm_out[:], warm_in[:], ACT.Copy)
-        ws_row, sx_row = 4, 8
-
-        def scale_loads(src, plane, row):
-            passes = src.shape[0]
-            return [
-                (
-                    plane[32 * q + row : 32 * q + row + 4, :].bitcast(I32).rearrange("r (z c) -> r z c", z=passes),
-                    src[:, 4 * q : 4 * q + 4, :].bitcast(I32).rearrange("z r c -> r z c"),
-                )
-                for q in range(4)
-            ]
-
-        def words(src):
-            return src.rearrange("p c t -> p (c t)").bitcast(I32)
 
         xf_planes = xf.rearrange("(a p t) n -> a t p n", p=P, t=PACK)
-        small = (
+        small_loads = (
             [(factor[:], fk.rearrange("(a p t) o -> p a (t o)", p=P, t=PACK))]
-            + scale_loads(ws_scales, rival_scales[:, :R], ws_row)
-            + scale_loads(sx_scales, rival_scales[:, R:], sx_row)
+            + scale_loads(ws_scales, rival_scales[:, :R], WS_ROW)
+            + scale_loads(sx_scales, rival_scales[:, R:], SX_ROW)
             + [(bias_col[:], bi.rearrange("o (p e) -> p (o e)", e=2))]
         )
-        behind = (1, 1, 1, 1, 2, 1, 1, 2)
-        at = 0
+        issued = 0
         for i in range(PLANES):
             nc.sync.dma_start(out=planes[i][:], in_=xf_planes[i // PACK, i % PACK])
             if i == 0:
                 nc.sync.dma_start(list_a[:], offs)
                 nc.sync.dma_start(list_b[:], offs2)
-            for dst, src in small[at : at + behind[i]]:
+            for dst, src in small_loads[issued : issued + SMALL_BEHIND_PLANE[i]]:
                 nc.sync.dma_start(out=dst, in_=src)
-            at = at + behind[i]
-        nc.sync.dma_start(out=ws_codes[:], in_=words(ws_words[0]))
-        nc.sync.dma_start(out=sx_codes[:], in_=words(sx_words[0]))
-        nc.sync.dma_start(out=w_codes[0][:], in_=words(w_words[0]))
-        for dst, src in scale_loads(w_scales, w_plane[:], 0):
+            issued = issued + SMALL_BEHIND_PLANE[i]
+        nc.sync.dma_start(out=ws_codes[:], in_=as_words(ws_words[0]))
+        nc.sync.dma_start(out=sx_codes[:], in_=as_words(sx_words[0]))
+        nc.sync.dma_start(out=w_codes[0][:], in_=as_words(w_words[0]))
+        for dst, src in scale_loads(w_scales, w_scale_tile[:], 0):
             nc.sync.dma_start(out=dst, in_=src)
-        nc.sync.dma_start(out=w_codes[1][:], in_=words(w_words[1]))
+        nc.sync.dma_start(out=w_codes[1][:], in_=as_words(w_words[1]))
         nc.sync.dma_start(out=wb_raw[:], in_=wb.rearrange("(p t) n -> p t n", t=PACK))
 
         bias_ps = psum.tile([P, 2, P], F32, name="bias_ps", tag="turn0")
@@ -108,13 +119,13 @@ def tile_list_largerpicks_rival_rowshares_kernel(
         nc.scalar.copy(out=bias_row[:], in_=bias_ps[:].rearrange("p e n -> p n e"))
 
         b_ps = [psum.tile([P, R], F32, name=f"b_ps{h}") for h in range(HALVES)]
-        for h in range(HALVES):
+        for h, cols in enumerate(halves):
             nc.tensor.matmul_mx(
                 out=b_ps[h][:],
-                lhsT=sx_codes[:, h * P : (h + 1) * P].bitcast(E4M3),
-                lhsT_scale=rival_scales[sx_row:, R + h * P : R + (h + 1) * P],
+                lhsT=sx_codes[:, cols].bitcast(E4M3),
+                lhsT_scale=rival_scales[SX_ROW:, R + cols.start : R + cols.stop],
                 rhs=ws_codes[:].bitcast(E4M3),
-                rhs_scale=rival_scales[ws_row:, :R],
+                rhs_scale=rival_scales[WS_ROW:, :R],
                 start=True,
                 stop=True,
             )
@@ -122,51 +133,50 @@ def tile_list_largerpicks_rival_rowshares_kernel(
         a_ps = [psum.tile([P, R], F32, name=f"a_ps{h}") for h in range(HALVES)]
         for a in range(PASSES):
             last_pass = a == PASSES - 1
-            col_cuts = [slice(h * P, (h + 1) * P) for h in range(HALVES)] if last_pass else [slice(0, J)]
+            pass_cuts = halves if last_pass else whole
             pick_a = keep.tile([P, PACK, J], F32, name=f"pick_a{a}")
             pick_b = keep.tile([P, PACK, J], F32, name=f"pick_b{a}")
             larger = keep.tile([P, PACK, J], F32, name=f"larger{a}")
-            woven = keep.tile([P, J, PACK], BF16, name=f"u_woven{a}", align_bytes=64)
+            u_woven = keep.tile([P, J, PACK], BF16, name=f"u_woven{a}", align_bytes=64)
             u_codes = keep.tile([P, J], I32, name=f"u_codes{a}", align_bytes=64)
             u_scales = keep.tile([P, J], U8, name=f"u_scales{a}", align_bytes=64)
             for t in range(PACK):
                 i = a * PACK + t
-                cuts = col_cuts if t == PACK - 1 else [slice(0, J)]
-                for cols in cuts:
-                    entries = slice(cols.start // 16, cols.stop // 16)
+                plane_cuts = pass_cuts if t == PACK - 1 else whole
+                for cols in plane_cuts:
+                    entries = slice(cols.start // LIST_ROWS, cols.stop // LIST_ROWS)
                     nc.scalar.activation(pick_a[:, t, cols], planes[i][:].indirect(list_a[:, entries]), ACT.Copy)
-                    if i in VECTOR_GATHERS and cols.start == 0:
+                    if i in VECTOR_GATHERS:
                         nc.vector.tensor_copy(pick_b[:, t, cols], planes[i][:].indirect(list_b[:, entries]))
                     else:
                         nc.scalar.activation(pick_b[:, t, cols], planes[i][:].indirect(list_b[:, entries]), ACT.Copy)
                 if t % 2 == 1:
                     pair = slice(t - 1, t + 1)
-                    for cols in cuts:
+                    for cols in plane_cuts:
                         nc.vector.tensor_tensor(
                             larger[:, pair, cols], pick_a[:, pair, cols], pick_b[:, pair, cols], ALU.max
                         )
-            for cols in col_cuts:
-                width = cols.stop - cols.start
+            for cols in pass_cuts:
+                runs = (cols.stop - cols.start) // RUN
                 nc.vector.tensor_tensor(
-                    woven[:, cols, :].rearrange("p (c i) t -> p c t i", i=RUN),
-                    larger[:, :, cols].rearrange("p t (c i) -> p c t i", i=RUN),
-                    factor[:, a, :].unsqueeze(1).unsqueeze(3).to_broadcast([P, width // RUN, PACK, RUN]),
+                    woven_order(u_woven[:, cols, :]),
+                    plane_order(larger[:, :, cols]),
+                    factor[:, a, :].unsqueeze(1).unsqueeze(3).to_broadcast([P, runs, PACK, RUN]),
                     ALU.mult,
                 )
-            for cols in col_cuts:
+            for cols in pass_cuts:
                 nc.vector.quantize_mx(
                     out=u_codes[:, cols].bitcast(E4M3),
                     scales=u_scales[:, cols],
-                    in_=woven[:, cols, :].rearrange("p c t -> p (c t)"),
+                    in_=u_woven[:, cols, :].rearrange("p c t -> p (c t)"),
                 )
-            for h in range(HALVES):
-                cols = slice(h * P, (h + 1) * P)
+            for h, cols in enumerate(halves):
                 nc.tensor.matmul_mx(
                     out=a_ps[h][:],
                     lhsT=u_codes[:, cols].bitcast(E4M3),
                     lhsT_scale=u_scales[:, cols],
                     rhs=w_codes[a][:].bitcast(E5M2),
-                    rhs_scale=w_plane[:, a * R : (a + 1) * R],
+                    rhs_scale=w_scale_tile[:, a * R : (a + 1) * R],
                     start=(a == 0),
                     stop=last_pass,
                 )
@@ -174,12 +184,14 @@ def tile_list_largerpicks_rival_rowshares_kernel(
         rival = []
         for h in range(HALVES):
             b_sb = keep.tile([P, 2, P, 2], F32, name=f"b_sb{h}")
-            nc.scalar.copy(out=b_sb[:], in_=b_ps[h][:].rearrange("j (p u e) -> j u p e", u=2, e=2))
+            nc.scalar.copy(out=b_sb[:], in_=b_ps[h][:].rearrange("j (p s e) -> j s p e", s=2, e=2))
             rival.append(b_sb)
 
         wb_woven = keep.tile([P, N, PACK], BF16, name="wb_woven", align_bytes=64)
-        weave(nc.vector.tensor_copy, wb_woven[:, : N // 2, :], wb_raw[:, :, : N // 2])
-        weave(nc.scalar.copy, wb_woven[:, N // 2 :, :], wb_raw[:, :, N // 2 :])
+        nc.vector.tensor_copy(
+            out=woven_order(wb_woven[:, : N // 2, :]), in_=plane_order(wb_raw[:, :, : N // 2])
+        )
+        nc.scalar.copy(out=woven_order(wb_woven[:, N // 2 :, :]), in_=plane_order(wb_raw[:, :, N // 2 :]))
         wb_codes = keep.tile([P, N], I32, name="wb_codes", align_bytes=64)
         wb_scales = keep.tile([P, N], U8, name="wb_scales", align_bytes=64)
 
@@ -187,18 +199,18 @@ def tile_list_largerpicks_rival_rowshares_kernel(
         for h in range(HALVES):
             hid = keep.tile([P, 2, P, 2], BF16, name=f"hid{h}")
             turned = psum.tile([P, 2, P], F32, name=f"turned{h}", tag=f"turn{h}")
-            a_view = a_ps[h][:].rearrange("j (p u e) -> j u p e", u=2, e=2)
-            for u in range(2):
-                nc.vector.tensor_tensor(hid[:, u], a_view[:, u], rival[h][:, u], ALU.max)
+            a_view = a_ps[h][:].rearrange("j (p s e) -> j s p e", s=2, e=2)
+            for s in range(2):
+                nc.vector.tensor_tensor(hid[:, s], a_view[:, s], rival[h][:, s], ALU.max)
                 nc.tensor.transpose(
-                    turned[:, u, :], hid[:, u].rearrange("j p e -> j (p e)").bitcast(F32), ident[:]
+                    turned[:, s, :], hid[:, s].rearrange("j p e -> j (p e)").bitcast(F32), ident[:]
                 )
-            hw = keep.tile([P, P * PACK], BF16, name=f"hid_woven{h}", align_bytes=64)
+            hid_half = keep.tile([P, P * PACK], BF16, name=f"hid_woven{h}", align_bytes=64)
             nc.scalar.copy(
-                out=hw[:].bitcast(F32).rearrange("p (j u) -> p j u", u=2),
-                in_=turned[:].rearrange("p u j -> p j u"),
+                out=hid_half[:].bitcast(F32).rearrange("p (j s) -> p j s", s=2),
+                in_=turned[:].rearrange("p s j -> p j s"),
             )
-            hid_woven.append(hw)
+            hid_woven.append(hid_half)
 
         nc.vector.quantize_mx(
             out=wb_codes[:].bitcast(E4M3), scales=wb_scales[:], in_=wb_woven[:].rearrange("p c t -> p (c t)")
@@ -209,9 +221,9 @@ def tile_list_largerpicks_rival_rowshares_kernel(
             hid_codes = keep.tile([P, P], I32, name=f"hid_codes{h}", align_bytes=64)
             hid_scales = keep.tile([P, P], U8, name=f"hid_scales{h}", align_bytes=64)
             nc.vector.quantize_mx(out=hid_codes[:].bitcast(E5M2), scales=hid_scales[:], in_=hid_woven[h][:])
-            pp = psum.tile([P, N], F32, name=f"p_ps{h}")
+            p_half = psum.tile([P, N], F32, name=f"p_ps{h}")
             nc.tensor.matmul_mx(
-                out=pp[:],
+                out=p_half[:],
                 lhsT=hid_codes[:].bitcast(E5M2),
                 lhsT_scale=hid_scales[:],
                 rhs=wb_codes[:].bitcast(E4M3),
@@ -219,9 +231,9 @@ def tile_list_largerpicks_rival_rowshares_kernel(
                 start=True,
                 stop=True,
             )
-            p_ps.append(pp)
+            p_ps.append(p_half)
 
-        for h in range(HALVES):
+        for h, rows in enumerate(halves):
             neg = keep.tile([P, N], F32, name=f"neg{h}")
             least = keep.tile([P, 1], F32, name=f"least{h}")
             ea = keep.tile([P, N], F32, name=f"ea{h}")
@@ -229,10 +241,15 @@ def tile_list_largerpicks_rival_rowshares_kernel(
             inv = keep.tile([P, 1], F32, name=f"inv{h}")
             shares = keep.tile([P, N], F32, name=f"shares{h}")
             nc.vector.scalar_tensor_tensor(
-                neg[:], p_ps[h][:], -0.7, bias_row[:].rearrange("p n e -> p (n e)"), ALU.mult, ALU.subtract
+                neg[:],
+                p_ps[h][:],
+                -LOGIT_SCALE,
+                bias_row[:].rearrange("p n e -> p (n e)"),
+                ALU.mult,
+                ALU.subtract,
             )
             nc.vector.tensor_reduce(least[:], neg[:], mybir.AxisListType.X, ALU.min)
             nc.scalar.activation(ea[:], neg[:], ACT.Exp, bias=least[:], scale=-1.0, accum_out=total[:])
             nc.vector.reciprocal(inv[:], total[:])
-            nc.vector.tensor_scalar(shares[:], ea[:], inv[:], 256.0, ALU.mult, ALU.mult)
-            nc.sync.dma_start(out=out[h * P : (h + 1) * P, :], in_=shares[:])
+            nc.vector.tensor_scalar(shares[:], ea[:], inv[:], SHARE_SUM, ALU.mult, ALU.mult)
+            nc.sync.dma_start(out=out[rows, :], in_=shares[:])

from contextlib import ExitStack

import concourse.mybir as mybir
from concourse.masks import make_identity

K, T, J, R, L, N = 1024, 1024, 256, 512, 512, 256
FLOPS = 2 * (K * R * J + L * R * J + R * J * N)
LOGIT_SCALE = 0.7
SHARE_SUM = 256.0

F32 = mybir.dt.float32
BF16 = mybir.dt.bfloat16
I32 = mybir.dt.int32
U16 = mybir.dt.uint16
U8 = mybir.dt.uint8
E4M3 = mybir.dt.float8_e4m3fn_x4
E5M2 = mybir.dt.float8_e5m2_x4
ALU = mybir.AluOpType
ACT = mybir.ActivationFunctionType

P = 128
PACK = 4
PASSES = K // (P * PACK)
PLANES = PASSES * PACK
HALVES = J // P
LIST_ROWS = 16
QUADRANTS = 4
WS_ROW, SX_ROW = 4, 8
RUN = 2
VECTOR_GATHERS = (0, 1, 2, 3, 6, 7)
SMALL_BEHIND_PLANE = (1, 1, 1, 1, 2, 1, 1, 2)


def woven_order(ap):
    return ap.rearrange("p (c i) t -> p c t i", i=RUN)


def plane_order(ap):
    return ap.rearrange("p t (c i) -> p c t i", i=RUN)


def as_words(codes):
    return codes.rearrange("p c t -> p (c t)").bitcast(I32)


def scale_loads(src, scale_tile, first_row):
    passes = src.shape[0]
    return [
        (
            scale_tile[32 * q + first_row : 32 * q + first_row + 4, :]
            .bitcast(I32)
            .rearrange("r (z c) -> r z c", z=passes),
            src[:, 4 * q : 4 * q + 4, :].bitcast(I32).rearrange("z r c -> r z c"),
        )
        for q in range(QUADRANTS)
    ]


def tile_list_largerpicks_rival_rowshares_kernel(
    tc, xf, fk, w_words, w_scales, sx_words, sx_scales, ws_words, ws_scales, wb, bi, offs, offs2, out
):
    nc = tc.nc
    halves = [slice(h * P, (h + 1) * P) for h in range(HALVES)]
    whole = [slice(0, J)]
    with ExitStack() as ctx:
        keep = ctx.enter_context(tc.tile_pool(name="keep", bufs=1))
        psum = ctx.enter_context(tc.psum_pool(name="psum", bufs=1))

        list_a = keep.tile([P, J // LIST_ROWS], U16, name="list_a")
        list_b = keep.tile([P, J // LIST_ROWS], U16, name="list_b")
        planes = [keep.tile([P, T], F32, name=f"plane{i}") for i in range(PLANES)]
        factor = keep.tile([P, PASSES, PACK], F32, name="factor")
        bias_col = keep.tile([P, 2], F32, name="bias_col")
        rival_scales = keep.tile([P, R + J], U8, name="rival_scales", align_bytes=64)
        w_scale_tile = keep.tile([P, PASSES * R], U8, name="w_scale_tile", align_bytes=64)
        w_codes = [keep.tile([P, R], I32, name=f"w_codes{a}", align_bytes=64) for a in range(PASSES)]
        ws_codes = keep.tile([P, R], I32, name="ws_codes", align_bytes=64)
        sx_codes = keep.tile([P, J], I32, name="sx_codes", align_bytes=64)
        wb_raw = keep.tile([P, PACK, N], F32, name="wb_raw")
        ident = keep.tile([P, P], F32, name="ident")

        nc.vector.memset(rival_scales[:].bitcast(I32), 0)
        nc.vector.memset(w_scale_tile[:].bitcast(I32), 0)
        make_identity(nc, ident[:])

        warm_in = keep.tile([P, 1], F32, name="warm_in")
        warm_out = keep.tile([P, 1], F32, name="warm_out")
        nc.vector.memset(warm_in[:], 0.0)
        nc.scalar.activation(warm_out[:], warm_in[:], ACT.Copy)

        xf_planes = xf.rearrange("(a p t) n -> a t p n", p=P, t=PACK)
        small_loads = (
            [(factor[:], fk.rearrange("(a p t) o -> p a (t o)", p=P, t=PACK))]
            + scale_loads(ws_scales, rival_scales[:, :R], WS_ROW)
            + scale_loads(sx_scales, rival_scales[:, R:], SX_ROW)
            + [(bias_col[:], bi.rearrange("o (p e) -> p (o e)", e=2))]
        )
        issued = 0
        for i in range(PLANES):
            nc.sync.dma_start(out=planes[i][:], in_=xf_planes[i // PACK, i % PACK])
            if i == 0:
                nc.sync.dma_start(list_a[:], offs)
                nc.sync.dma_start(list_b[:], offs2)
            for dst, src in small_loads[issued : issued + SMALL_BEHIND_PLANE[i]]:
                nc.sync.dma_start(out=dst, in_=src)
            issued = issued + SMALL_BEHIND_PLANE[i]
        nc.sync.dma_start(out=ws_codes[:], in_=as_words(ws_words[0]))
        nc.sync.dma_start(out=sx_codes[:], in_=as_words(sx_words[0]))
        nc.sync.dma_start(out=w_codes[0][:], in_=as_words(w_words[0]))
        for dst, src in scale_loads(w_scales, w_scale_tile[:], 0):
            nc.sync.dma_start(out=dst, in_=src)
        nc.sync.dma_start(out=w_codes[1][:], in_=as_words(w_words[1]))
        nc.sync.dma_start(out=wb_raw[:], in_=wb.rearrange("(p t) n -> p t n", t=PACK))

        bias_ps = psum.tile([P, 2, P], F32, name="bias_ps", tag="turn0")
        for e in range(2):
            nc.tensor.transpose(bias_ps[:, e, :], bias_col[:, e : e + 1].to_broadcast([P, P]), ident[:])
        bias_row = keep.tile([P, P, 2], F32, name="bias_row")
        nc.scalar.copy(out=bias_row[:], in_=bias_ps[:].rearrange("p e n -> p n e"))

        b_ps = [psum.tile([P, R], F32, name=f"b_ps{h}") for h in range(HALVES)]
        for h, cols in enumerate(halves):
            nc.tensor.matmul_mx(
                out=b_ps[h][:],
                lhsT=sx_codes[:, cols].bitcast(E4M3),
                lhsT_scale=rival_scales[SX_ROW:, R + cols.start : R + cols.stop],
                rhs=ws_codes[:].bitcast(E4M3),
                rhs_scale=rival_scales[WS_ROW:, :R],
                start=True,
                stop=True,
            )

        a_ps = [psum.tile([P, R], F32, name=f"a_ps{h}") for h in range(HALVES)]
        for a in range(PASSES):
            last_pass = a == PASSES - 1
            pass_cuts = halves if last_pass else whole
            pick_a = keep.tile([P, PACK, J], F32, name=f"pick_a{a}")
            pick_b = keep.tile([P, PACK, J], F32, name=f"pick_b{a}")
            larger = keep.tile([P, PACK, J], F32, name=f"larger{a}")
            u_woven = keep.tile([P, J, PACK], BF16, name=f"u_woven{a}", align_bytes=64)
            u_codes = keep.tile([P, J], I32, name=f"u_codes{a}", align_bytes=64)
            u_scales = keep.tile([P, J], U8, name=f"u_scales{a}", align_bytes=64)
            for t in range(PACK):
                i = a * PACK + t
                plane_cuts = pass_cuts if t == PACK - 1 else whole
                for cols in plane_cuts:
                    entries = slice(cols.start // LIST_ROWS, cols.stop // LIST_ROWS)
                    nc.scalar.activation(pick_a[:, t, cols], planes[i][:].indirect(list_a[:, entries]), ACT.Copy)
                    if i in VECTOR_GATHERS:
                        nc.vector.tensor_copy(pick_b[:, t, cols], planes[i][:].indirect(list_b[:, entries]))
                    else:
                        nc.scalar.activation(pick_b[:, t, cols], planes[i][:].indirect(list_b[:, entries]), ACT.Copy)
                if t % 2 == 1:
                    pair = slice(t - 1, t + 1)
                    for cols in plane_cuts:
                        nc.vector.tensor_tensor(
                            larger[:, pair, cols], pick_a[:, pair, cols], pick_b[:, pair, cols], ALU.max
                        )
            for cols in pass_cuts:
                runs = (cols.stop - cols.start) // RUN
                nc.vector.tensor_tensor(
                    woven_order(u_woven[:, cols, :]),
                    plane_order(larger[:, :, cols]),
                    factor[:, a, :].unsqueeze(1).unsqueeze(3).to_broadcast([P, runs, PACK, RUN]),
                    ALU.mult,
                )
            for cols in pass_cuts:
                nc.vector.quantize_mx(
                    out=u_codes[:, cols].bitcast(E4M3),
                    scales=u_scales[:, cols],
                    in_=u_woven[:, cols, :].rearrange("p c t -> p (c t)"),
                )
            for h, cols in enumerate(halves):
                nc.tensor.matmul_mx(
                    out=a_ps[h][:],
                    lhsT=u_codes[:, cols].bitcast(E4M3),
                    lhsT_scale=u_scales[:, cols],
                    rhs=w_codes[a][:].bitcast(E5M2),
                    rhs_scale=w_scale_tile[:, a * R : (a + 1) * R],
                    start=(a == 0),
                    stop=last_pass,
                )

        rival = []
        for h in range(HALVES):
            b_sb = keep.tile([P, 2, P, 2], F32, name=f"b_sb{h}")
            nc.scalar.copy(out=b_sb[:], in_=b_ps[h][:].rearrange("j (p s e) -> j s p e", s=2, e=2))
            rival.append(b_sb)

        wb_woven = keep.tile([P, N, PACK], BF16, name="wb_woven", align_bytes=64)
        nc.vector.tensor_copy(
            out=woven_order(wb_woven[:, : N // 2, :]), in_=plane_order(wb_raw[:, :, : N // 2])
        )
        nc.scalar.copy(out=woven_order(wb_woven[:, N // 2 :, :]), in_=plane_order(wb_raw[:, :, N // 2 :]))
        wb_codes = keep.tile([P, N], I32, name="wb_codes", align_bytes=64)
        wb_scales = keep.tile([P, N], U8, name="wb_scales", align_bytes=64)

        hid_woven = []
        for h in range(HALVES):
            hid = keep.tile([P, 2, P, 2], BF16, name=f"hid{h}")
            turned = psum.tile([P, 2, P], F32, name=f"turned{h}", tag=f"turn{h}")
            a_view = a_ps[h][:].rearrange("j (p s e) -> j s p e", s=2, e=2)
            for s in range(2):
                nc.vector.tensor_tensor(hid[:, s], a_view[:, s], rival[h][:, s], ALU.max)
                nc.tensor.transpose(
                    turned[:, s, :], hid[:, s].rearrange("j p e -> j (p e)").bitcast(F32), ident[:]
                )
            hid_half = keep.tile([P, P * PACK], BF16, name=f"hid_woven{h}", align_bytes=64)
            nc.scalar.copy(
                out=hid_half[:].bitcast(F32).rearrange("p (j s) -> p j s", s=2),
                in_=turned[:].rearrange("p s j -> p j s"),
            )
            hid_woven.append(hid_half)

        nc.vector.quantize_mx(
            out=wb_codes[:].bitcast(E4M3), scales=wb_scales[:], in_=wb_woven[:].rearrange("p c t -> p (c t)")
        )

        p_ps = []
        for h in range(HALVES):
            hid_codes = keep.tile([P, P], I32, name=f"hid_codes{h}", align_bytes=64)
            hid_scales = keep.tile([P, P], U8, name=f"hid_scales{h}", align_bytes=64)
            nc.vector.quantize_mx(out=hid_codes[:].bitcast(E5M2), scales=hid_scales[:], in_=hid_woven[h][:])
            p_half = psum.tile([P, N], F32, name=f"p_ps{h}")
            nc.tensor.matmul_mx(
                out=p_half[:],
                lhsT=hid_codes[:].bitcast(E5M2),
                lhsT_scale=hid_scales[:],
                rhs=wb_codes[:].bitcast(E4M3),
                rhs_scale=wb_scales[:],
                start=True,
                stop=True,
            )
            p_ps.append(p_half)

        for h, rows in enumerate(halves):
            neg = keep.tile([P, N], F32, name=f"neg{h}")
            least = keep.tile([P, 1], F32, name=f"least{h}")
            ea = keep.tile([P, N], F32, name=f"ea{h}")
            total = keep.tile([P, 1], F32, name=f"total{h}")
            inv = keep.tile([P, 1], F32, name=f"inv{h}")
            shares = keep.tile([P, N], F32, name=f"shares{h}")
            nc.vector.scalar_tensor_tensor(
                neg[:],
                p_ps[h][:],
                -LOGIT_SCALE,
                bias_row[:].rearrange("p n e -> p (n e)"),
                ALU.mult,
                ALU.subtract,
            )
            nc.vector.tensor_reduce(least[:], neg[:], mybir.AxisListType.X, ALU.min)
            nc.scalar.activation(ea[:], neg[:], ACT.Exp, bias=least[:], scale=-1.0, accum_out=total[:])
            nc.vector.reciprocal(inv[:], total[:])
            nc.vector.tensor_scalar(shares[:], ea[:], inv[:], SHARE_SUM, ALU.mult, ALU.mult)
            nc.sync.dma_start(out=out[rows, :], in_=shares[:])
